import numpy as np
import ml_dtypes


def mxq(x, axis, fmt="e4m3"):
    dtype, down = {"e4m3": (ml_dtypes.float8_e4m3fn, 7), "e5m2": (ml_dtypes.float8_e5m2, 14)}[fmt]
    v = np.moveaxis(np.asarray(x, np.float32).astype(ml_dtypes.bfloat16).astype(np.float64), axis, -1)
    blocks = v.reshape(v.shape[:-1] + (-1, 32))
    amax = np.abs(blocks).max(-1, keepdims=True)
    byte = np.maximum(np.where(amax > 0, np.frexp(amax)[1] - 1 + 127, 0) - down, 1)
    scale = np.exp2(byte - 127.0)
    codes = (blocks / scale).astype(np.float32).astype(dtype).astype(np.float64)
    return np.moveaxis((codes * scale).reshape(v.shape), -1, axis)


WIDE = False


def mx_kscale(k):
    if not WIDE:
        return np.ones(k)
    levels = np.array([10, -10, 5, -5, 0])
    if k % 512:
        return np.exp2(np.random.permutation(np.resize(levels, k // 32))).repeat(32)
    a = np.empty((k // 512, 16))
    for p in range(k // 512):
        a[p, :8] = np.random.permutation(np.resize(levels, 8))
        for g in range(8):
            far = levels[np.abs(levels - a[p, g]) >= 10]
            a[p, g + 8] = far[np.random.randint(len(far))]
    return np.exp2(a.ravel()).repeat(32)


def f64(x):
    return np.asarray(x).astype(np.float64)


def striped(idx):
    return np.tile(idx.reshape(-1, 16).T, (8, 1)).astype(np.uint16)


def unstriped(offs):
    return offs[:16].T.reshape(-1).astype(np.int64)


E2M1 = np.array([0.0, 0.5, 1.0, 1.5, 2.0, 3.0, 4.0, 6.0, -0.0, -0.5, -1.0, -1.5, -2.0, -3.0, -4.0, -6.0])


def pack_weight(w, fmt):
    k, n = w.shape
    w = f64(np.asarray(w, np.float32).astype(ml_dtypes.bfloat16)).reshape(k // 32, 32, n)
    amax = np.abs(w).max(1)
    if fmt == "e4m3":
        byte = np.frexp(amax)[1] - 1 + 127 - 7
    else:
        mant, ex = np.frexp(amax / 6.0)
        byte = np.where(mant > 0.5, ex, ex - 1) + 127
    byte = np.clip(np.where(amax > 0, byte, 1), 1, 254)
    scaled = (w * np.exp2(127.0 - byte)[:, None, :]).reshape(k, n).astype(np.float32)
    by_word = np.ascontiguousarray(scaled.reshape(k // 512, 128, 4, n).transpose(0, 1, 3, 2))
    if fmt == "e4m3":
        words = by_word.astype(ml_dtypes.float8_e4m3fn).view(np.uint8)
    else:
        c = by_word.astype(ml_dtypes.float4_e2m1fn).view(np.uint8) & 0xF
        words = (c[..., 0::2] | (c[..., 1::2] << 4)).reshape(k // 512, 128, 2 * n)
    return np.ascontiguousarray(words), np.ascontiguousarray(byte.astype(np.uint8).reshape(k // 512, 16, n))


def unpack_weight(words, scales, fmt):
    g, _, n = scales.shape
    words = np.ascontiguousarray(words).reshape(g, 128, n, -1)
    if fmt == "e4m3":
        vals = words.view(ml_dtypes.float8_e4m3fn).astype(np.float64)
    else:
        nib = np.empty((g, 128, n, 4), np.uint8)
        nib[..., 0::2] = words & 0xF
        nib[..., 1::2] = words >> 4
        vals = E2M1[nib]
    vals = vals * np.repeat(np.exp2(scales.astype(np.float64) - 127.0), 8, axis=1)[..., None]
    return vals.transpose(0, 1, 3, 2).reshape(g * 512, n)


def d_silu(v):
    s = 1.0 / (1.0 + np.exp(-np.maximum(v, -700.0)))
    return s * (1.0 + v * (1.0 - s))


K, T, E, C, H, N = 384, 640, 2, 256, 512, 2048


def by_expert(wq, xq):
    return np.concatenate([wq[e].T @ xq[:, e * C:(e + 1) * C] for e in range(E)], axis=1)


def setup_inputs():
    n = np.random.standard_normal
    s = mx_kscale(N)[:, None]
    u = mx_kscale(H)
    w2 = [pack_weight(m, "e2m1") for m in n((E, N, H)) / np.sqrt(N) / s[None] * u[None, None, :]]
    w1 = [pack_weight(m, "e2m1") for m in n((E, H, K)) / np.sqrt(H) / u[None, :, None]]
    return {
        "dyT": (n((N, T)) * s).astype(np.float32),
        "a": n((H, E * C)).astype(np.float32),
        "w2_words": np.stack([m[0] for m in w2]),
        "w2_scales": np.stack([m[1] for m in w2]),
        "w1_words": np.stack([m[0] for m in w1]),
        "w1_scales": np.stack([m[1] for m in w1]),
        "gate": np.tile(np.random.uniform(0.2, 1.0, E * C), (N, 1)).astype(np.float32),
        "offs": striped(np.random.permutation(T)[:E * C]),
    }


def reference(dyT, a, w2_words, w2_scales, w1_words, w1_scales, gate, offs):
    idx = unstriped(offs)
    w2 = np.stack([unpack_weight(w2_words[e], w2_scales[e], "e2m1") for e in range(E)])
    w1 = np.stack([unpack_weight(w1_words[e], w1_scales[e], "e2m1") for e in range(E)])
    gq = mxq(f64(gate) * f64(dyT)[:, idx], 0, "e4m3")
    dh = by_expert(w2, gq)
    da = dh * d_silu(f64(a))
    dx = by_expert(w1, mxq(da, 0, "e4m3"))
    out = np.zeros((K, T))
    out[:, idx] = dx
    return out

@@ -1,0 +1,223 @@
+from contextlib import ExitStack
+
+import concourse.mybir as mybir
+from concourse.masks import make_identity
+
+F32 = mybir.dt.float32
+BF16 = mybir.dt.bfloat16
+I32 = mybir.dt.int32
+U32 = mybir.dt.uint32
+U16 = mybir.dt.uint16
+U8 = mybir.dt.uint8
+FP8X4 = mybir.dt.float8_e4m3fn_x4
+FP4X4 = mybir.dt.float4_e2m1fn_x4
+
+P = 128
+K, T, E, C, H, N = 384, 640, 2, 256, 512, 2048
+S = E * C
+PASSES = N // 512
+BLOCKS = S // P
+K_TILES = K // P
+FLOPS = 2 * S * H * (N + K)
+
+MULT = mybir.AluOpType.mult
+SUBTRACT = mybir.AluOpType.subtract
+SIGMOID = mybir.ActivationFunctionType.Sigmoid
+SILU = mybir.ActivationFunctionType.Silu
+
+
+def tile_moe_bdx_mlp_silu_kernel(
+    tc, dyT, a, w2_words, w2_scales, w1_words, w1_scales, gate, offs, out
+):
+    nc = tc.nc
+    with ExitStack() as ctx:
+        lists = ctx.enter_context(tc.tile_pool(name="lists", bufs=1))
+        keep = ctx.enter_context(tc.tile_pool(name="keep", bufs=1))
+        sums = ctx.enter_context(tc.psum_pool(name="sums", bufs=1))
+        work = ctx.enter_context(tc.psum_pool(name="work", bufs=4))
+
+        offsets = lists.tile([P, S // 16], U16, name="offsets")
+
+        def flat_i32(tile):
+            return tile[:].rearrange("p a n -> p (a n)").bitcast(I32)
+
+        w2_planes = keep.tile([P, E * PASSES, H], U8, name="w2_planes", align_bytes=64)
+        w1_planes = keep.tile([P, E, K], U8, name="w1_planes", align_bytes=64)
+        warm = keep.tile([P, 1], F32, name="warm")
+        warmed = keep.tile([P, 1], F32, name="warmed")
+        gates = keep.tile([P, S], F32, name="gates")
+        identity = keep.tile([P, P], F32, name="identity")
+        dy = [[keep.tile([P, T], F32, name=f"dy{s}{t}") for t in range(4)] for s in range(PASSES)]
+        windows = [keep.tile([P, T], F32, name=f"window{k}") for k in range(K_TILES)]
+        w2 = keep.tile([P, E * PASSES, 2 * H], U8, name="w2", align_bytes=64)
+        w1 = keep.tile([P, E, 2 * K], U8, name="w1", align_bytes=64)
+        a_sb = keep.tile([P, 4, S], F32, name="a_sb")
+
+        dy_rows = dyT.rearrange("(s p t) w -> s t p w", p=P, t=4)
+
+        def load_dy(s):
+            for t in range(4):
+                nc.sync.dma_start(out=dy[s][t][:], in_=dy_rows[s, t])
+
+        nc.vector.memset(flat_i32(w2_planes), 0)
+        nc.vector.memset(flat_i32(w1_planes), 0)
+        nc.vector.memset(warm[:], 0.0)
+        nc.scalar.activation(warmed[:], warm[:], SIGMOID)
+        for k in range(K_TILES):
+            nc.vector.memset(windows[k][:], 0.0)
+        make_identity(nc, identity[:])
+
+        nc.sync.dma_start(offsets[:], offs)
+        for e in range(E):
+            nc.scalar.dma_start(out=gates[:, e * C : (e + 1) * C], in_=gate[0:P, e * C : (e + 1) * C])
+        load_dy(0)
+        load_dy(1)
+        w2_planes_i32 = flat_i32(w2_planes).rearrange("p (a n) -> p a n", a=E * PASSES)
+        w1_planes_i32 = flat_i32(w1_planes).rearrange("p (a n) -> p a n", a=E)
+        w2_rows = w2_scales.rearrange("e s f i -> f (e s) i")
+        w1_rows = w1_scales.rearrange("e s f i -> f (e s) i")
+        for q in range(4):
+            nc.sync.dma_start(out=w2_planes_i32[32 * q : 32 * q + 4], in_=w2_rows[4 * q : 4 * q + 4].bitcast(I32))
+        w2_i32 = flat_i32(w2).rearrange("p (a n) -> p a n", a=E * PASSES)
+        for e in range(E):
+            nc.sync.dma_start(
+                out=w2_i32[:, e * PASSES : (e + 1) * PASSES, :],
+                in_=w2_words[e].rearrange("s p b -> p s b").bitcast(I32),
+            )
+        load_dy(2)
+        nc.sync.dma_start(out=a_sb[:], in_=a.rearrange("(b p) c -> p b c", p=P))
+        load_dy(3)
+        nc.sync.dma_start(
+            out=flat_i32(w1).rearrange("p (a n) -> p a n", a=E),
+            in_=w1_words.rearrange("e s p b -> p (e s) b").bitcast(I32),
+        )
+        for q in range(4):
+            nc.sync.dma_start(out=w1_planes_i32[32 * q : 32 * q + 4], in_=w1_rows[4 * q : 4 * q + 4].bitcast(I32))
+
+        g = [keep.tile([P, 4, S], F32, name=f"g{s}") for s in range(PASSES)]
+        g_bf = [keep.tile([P, S, 4], BF16, name=f"g_bf{s}", align_bytes=64) for s in range(PASSES)]
+        g_codes = [keep.tile([P, S], U32, name=f"g_codes{s}", align_bytes=64) for s in range(PASSES)]
+        g_planes = [keep.tile([P, S], U8, name=f"g_planes{s}", align_bytes=64) for s in range(PASSES)]
+        dh = [sums.tile([P, H], F32, name=f"dh{b}") for b in range(BLOCKS)]
+
+        def gather(s, lo, hi, tiles=range(4)):
+            for t in tiles:
+                nc.vector.tensor_tensor(
+                    g[s][:, t, lo:hi],
+                    dy[s][t][:].indirect(offsets[:, lo // 16 : hi // 16]),
+                    gates[:, lo:hi],
+                    MULT,
+                )
+
+        def interleave(s, lo, hi):
+            nc.scalar.copy(g_bf[s][:, lo:hi, :], g[s][:, :, lo:hi].rearrange("p t c -> p c t"))
+
+        def first_product(s, lo, hi):
+            nc.vector.quantize_mx(
+                out=g_codes[s][:, lo:hi].bitcast(FP8X4),
+                scales=g_planes[s][:, lo:hi],
+                in_=g_bf[s][:, lo:hi, :].rearrange("p c t -> p (c t)"),
+            )
+            for b in range(lo // P, hi // P):
+                e = b * P // C
+                nc.tensor.matmul_mx(
+                    out=dh[b][:],
+                    lhsT=g_codes[s][:, b * P : (b + 1) * P].bitcast(FP8X4),
+                    lhsT_scale=g_planes[s][:, b * P : (b + 1) * P],
+                    rhs=w2[:, e * PASSES + s, :].bitcast(FP4X4),
+                    rhs_scale=w2_planes[:, e * PASSES + s, :],
+                    start=(s == 0),
+                    stop=(s == PASSES - 1),
+                )
+
+        r = [keep.tile([P, H], F32, name=f"sig{b}") for b in range(BLOCKS)]
+        w = [keep.tile([P, H], F32, name=f"silu{b}") for b in range(BLOCKS)]
+        m = [keep.tile([P, H], F32, name=f"mix{b}") for b in range(BLOCKS)]
+        aT = []
+
+        def derivative_functions():
+            for b in range(BLOCKS):
+                turned = work.tile([P, 512], F32, name="turned")
+                aT.append(turned)
+                for i in range(4):
+                    nc.tensor.transpose(turned[:, i * P : (i + 1) * P], a_sb[:, i, b * P : (b + 1) * P], identity[:])
+                nc.scalar.activation(r[b][:], turned[:], SIGMOID)
+            for b in range(BLOCKS):
+                nc.scalar.activation(w[b][:], aT[b][:], SILU, scale=-1.0)
+
+        def derivative_products(lo, hi):
+            for b in range(lo, hi):
+                nc.vector.scalar_tensor_tensor(m[b][:], w[b][:], 1.0, r[b][:], SUBTRACT, MULT)
+
+        da = [keep.tile([P, H], BF16, name=f"da{b}", align_bytes=64) for b in range(BLOCKS)]
+        da_bf = keep.tile([P, S, 4], BF16, name="da_bf", align_bytes=64)
+        da_codes = keep.tile([P, S], U32, name="da_codes", align_bytes=64)
+        da_planes = keep.tile([P, S], U8, name="da_planes", align_bytes=64)
+        dx = [keep.tile([P, S], F32, name=f"dx{k}") for k in range(K_TILES)]
+
+        def hidden_gradient(b):
+            nc.vector.scalar_tensor_tensor(da[b][:], dh[b][:], -1.0, m[b][:], MULT, MULT)
+            turned = work.tile([P, 512], F32, name="turned")
+            words = da[b][:].bitcast(F32)
+            for u in range(2):
+                nc.tensor.transpose(turned[:, u * P : (u + 1) * P], words[:, u : 2 * P : 2], identity[:])
+            nc.scalar.copy(
+                da_bf[:, b * P : (b + 1) * P, :].rearrange("p c t -> p (c t)").bitcast(F32).rearrange("p (r u) -> p r u", u=2),
+                turned[:, 0 : 2 * P].rearrange("p (u r) -> p r u", u=2),
+            )
+
+        def second_product(lo, hi):
+            e = lo // C
+            nc.vector.quantize_mx(
+                out=da_codes[:, lo:hi].bitcast(FP8X4),
+                scales=da_planes[:, lo:hi],
+                in_=da_bf[:, lo:hi, :].rearrange("p c t -> p (c t)"),
+            )
+            for k in range(K_TILES):
+                product = work.tile([P, 512], F32, name="turned")
+                nc.tensor.matmul_mx(
+                    out=product[:, 0 : hi - lo],
+                    lhsT=w1[:, e, 2 * P * k : 2 * P * (k + 1)].bitcast(FP4X4),
+                    lhsT_scale=w1_planes[:, e, P * k : P * (k + 1)],
+                    rhs=da_codes[:, lo:hi].bitcast(FP8X4),
+                    rhs_scale=da_planes[:, lo:hi],
+                    start=True,
+                    stop=True,
+                )
+                nc.scalar.copy(dx[k][:, lo:hi], product[:, 0 : hi - lo])
+
+        def scatter(lo, hi, k):
+            nc.vector.tensor_copy(windows[k][:].indirect(offsets[:, lo // 16 : hi // 16]), dx[k][:, lo:hi])
+
+        gather(0, 0, C, [0])
+        gather(0, C, S, [0])
+        gather(0, 0, S, [1, 2, 3])
+        interleave(0, 0, S)
+        gather(1, 0, S)
+        interleave(1, 0, S)
+        first_product(0, 0, S)
+        derivative_functions()
+        gather(2, 0, S)
+        interleave(2, 0, C)
+        interleave(2, C, S)
+        first_product(1, 0, S)
+        gather(3, 0, C)
+        interleave(3, 0, C)
+        first_product(2, 0, S)
+        derivative_products(0, 2)
+        gather(3, C, S)
+        interleave(3, C, S)
+        first_product(3, 0, C)
+        hidden_gradient(0)
+        hidden_gradient(1)
+        first_product(3, C, S)
+        second_product(0, C)
+        derivative_products(2, 4)
+        hidden_gradient(2)
+        hidden_gradient(3)
+        second_product(C, S)
+        for k in range(K_TILES):
+            scatter(0, C, k)
+        for k in range(K_TILES):
+            scatter(C, S, k)
+            nc.sync.dma_start(out=out[k * P : (k + 1) * P, :], in_=windows[k][:])

@@ -23,6 +23,7 @@ FLOPS = 2 * S * H * (N + K)
 MULT = mybir.AluOpType.mult
 SUBTRACT = mybir.AluOpType.subtract
 SIGMOID = mybir.ActivationFunctionType.Sigmoid
+COPY = mybir.ActivationFunctionType.Copy
 SILU = mybir.ActivationFunctionType.Silu
 
 
@@ -44,6 +45,7 @@ def tile_moe_bdx_mlp_silu_kernel(
         w2_planes = keep.tile([P, E * PASSES, H], U8, name="w2_planes", align_bytes=64)
         w1_planes = keep.tile([P, E, K], U8, name="w1_planes", align_bytes=64)
         warm = keep.tile([P, 1], F32, name="warm")
+        zero = keep.tile([P, 1], F32, name="zero")
         warmed = keep.tile([P, 1], F32, name="warmed")
         gates = keep.tile([P, S], F32, name="gates")
         identity = keep.tile([P, P], F32, name="identity")
@@ -55,44 +57,47 @@ def tile_moe_bdx_mlp_silu_kernel(
 
         dy_rows = dyT.rearrange("(s p t) w -> s t p w", p=P, t=4)
 
-        def load_dy(s):
-            for t in range(4):
+        def load_dy(s, rows=range(4)):
+            for t in rows:
                 nc.sync.dma_start(out=dy[s][t][:], in_=dy_rows[s, t])
 
+        nc.sync.dma_start(offsets[:], offs)
+        nc.sync.dma_start(out=gates[:, 0:C], in_=gate[0:P, 0:C])
+        load_dy(0, [0])
+        nc.sync.dma_start(out=gates[:, C:S], in_=gate[0:P, C:S])
+        load_dy(0, [1, 2, 3])
+        load_dy(1, [0, 1])
+        nc.sync.dma_start(out=a_sb[:], in_=a.rearrange("(b p) c -> p b c", p=P))
+        load_dy(1, [2, 3])
+        load_dy(2)
+        load_dy(3)
+
+        nc.gpsimd.memset(warm[:], 0.0)
+        nc.scalar.activation(warmed[:], warm[:], SIGMOID)
+        make_identity(nc, identity[:])
         nc.vector.memset(flat_i32(w2_planes), 0)
         nc.vector.memset(flat_i32(w1_planes), 0)
-        nc.vector.memset(warm[:], 0.0)
-        nc.scalar.activation(warmed[:], warm[:], SIGMOID)
         for k in range(K_TILES):
             nc.vector.memset(windows[k][:], 0.0)
-        make_identity(nc, identity[:])
 
-        nc.sync.dma_start(offsets[:], offs)
-        for e in range(E):
-            nc.scalar.dma_start(out=gates[:, e * C : (e + 1) * C], in_=gate[0:P, e * C : (e + 1) * C])
-        load_dy(0)
-        load_dy(1)
         w2_planes_i32 = flat_i32(w2_planes).rearrange("p (a n) -> p a n", a=E * PASSES)
         w1_planes_i32 = flat_i32(w1_planes).rearrange("p (a n) -> p a n", a=E)
         w2_rows = w2_scales.rearrange("e s f i -> f (e s) i")
         w1_rows = w1_scales.rearrange("e s f i -> f (e s) i")
         for q in range(4):
             nc.sync.dma_start(out=w2_planes_i32[32 * q : 32 * q + 4], in_=w2_rows[4 * q : 4 * q + 4].bitcast(I32))
+        for q in range(4):
+            nc.sync.dma_start(out=w1_planes_i32[32 * q : 32 * q + 4], in_=w1_rows[4 * q : 4 * q + 4].bitcast(I32))
         w2_i32 = flat_i32(w2).rearrange("p (a n) -> p a n", a=E * PASSES)
         for e in range(E):
             nc.sync.dma_start(
                 out=w2_i32[:, e * PASSES : (e + 1) * PASSES, :],
                 in_=w2_words[e].rearrange("s p b -> p s b").bitcast(I32),
             )
-        load_dy(2)
-        nc.sync.dma_start(out=a_sb[:], in_=a.rearrange("(b p) c -> p b c", p=P))
-        load_dy(3)
         nc.sync.dma_start(
             out=flat_i32(w1).rearrange("p (a n) -> p a n", a=E),
             in_=w1_words.rearrange("e s p b -> p (e s) b").bitcast(I32),
         )
-        for q in range(4):
-            nc.sync.dma_start(out=w1_planes_i32[32 * q : 32 * q + 4], in_=w1_rows[4 * q : 4 * q + 4].bitcast(I32))
 
         g = [keep.tile([P, 4, S], F32, name=f"g{s}") for s in range(PASSES)]
         g_bf = [keep.tile([P, S, 4], BF16, name=f"g_bf{s}", align_bytes=64) for s in range(PASSES)]
@@ -142,8 +147,9 @@ def tile_moe_bdx_mlp_silu_kernel(
                 for i in range(4):
                     nc.tensor.transpose(turned[:, i * P : (i + 1) * P], a_sb[:, i, b * P : (b + 1) * P], identity[:])
                 nc.scalar.activation(r[b][:], turned[:], SIGMOID)
+            nc.scalar.activation(zero[:], r[BLOCKS - 1][:, 0:1], COPY, scale=0.0)
             for b in range(BLOCKS):
-                nc.scalar.activation(w[b][:], aT[b][:], SILU, scale=-1.0)
+                nc.scalar.activation(w[b][:], aT[b][:], SILU, scale=-1.0, bias=zero[:])
 
         def derivative_products(lo, hi):
             for b in range(lo, hi):
@@ -193,25 +199,24 @@ def tile_moe_bdx_mlp_silu_kernel(
         gather(0, C, S, [0])
         gather(0, 0, S, [1, 2, 3])
         interleave(0, 0, S)
+        derivative_functions()
         gather(1, 0, S)
         interleave(1, 0, S)
         first_product(0, 0, S)
-        derivative_functions()
         gather(2, 0, S)
-        interleave(2, 0, C)
-        interleave(2, C, S)
+        interleave(2, 0, S)
         first_product(1, 0, S)
         gather(3, 0, C)
         interleave(3, 0, C)
         first_product(2, 0, S)
-        derivative_products(0, 2)
-        gather(3, C, S)
-        interleave(3, C, S)
         first_product(3, 0, C)
+        derivative_products(0, 2)
         hidden_gradient(0)
         hidden_gradient(1)
-        first_product(3, C, S)
         second_product(0, C)
+        gather(3, C, S)
+        interleave(3, C, S)
+        first_product(3, C, S)
         derivative_products(2, 4)
         hidden_gradient(2)
         hidden_gradient(3)

@@ -115,7 +115,10 @@ def tile_moe_bdx_mlp_silu_kernel(
                 )
 
         def interleave(s, lo, hi):
-            nc.scalar.copy(g_bf[s][:, lo:hi, :], g[s][:, :, lo:hi].rearrange("p t c -> p c t"))
+            nc.scalar.copy(
+                g_bf[s][:, lo:hi, :].rearrange("p (c i) t -> p c t i", i=4),
+                g[s][:, :, lo:hi].rearrange("p t (c i) -> p c t i", i=4),
+            )
 
         def first_product(s, lo, hi):
             nc.vector.quantize_mx(

from contextlib import ExitStack

import concourse.mybir as mybir
from concourse.masks import make_identity

F32 = mybir.dt.float32
BF16 = mybir.dt.bfloat16
I32 = mybir.dt.int32
U32 = mybir.dt.uint32
U16 = mybir.dt.uint16
U8 = mybir.dt.uint8
FP8X4 = mybir.dt.float8_e4m3fn_x4
FP4X4 = mybir.dt.float4_e2m1fn_x4

P = 128
K, T, E, C, H, N = 384, 640, 2, 256, 512, 2048
S = E * C
PASSES = N // 512
BLOCKS = S // P
K_TILES = K // P
FLOPS = 2 * S * H * (N + K)

MULT = mybir.AluOpType.mult
SUBTRACT = mybir.AluOpType.subtract
SIGMOID = mybir.ActivationFunctionType.Sigmoid
COPY = mybir.ActivationFunctionType.Copy
SILU = mybir.ActivationFunctionType.Silu


def tile_moe_bdx_mlp_silu_kernel(
    tc, dyT, a, w2_words, w2_scales, w1_words, w1_scales, gate, offs, out
):
    nc = tc.nc
    with ExitStack() as ctx:
        lists = ctx.enter_context(tc.tile_pool(name="lists", bufs=1))
        keep = ctx.enter_context(tc.tile_pool(name="keep", bufs=1))
        sums = ctx.enter_context(tc.psum_pool(name="sums", bufs=1))
        work = ctx.enter_context(tc.psum_pool(name="work", bufs=4))

        offsets = lists.tile([P, S // 16], U16, name="offsets")

        def flat_i32(tile):
            return tile[:].rearrange("p a n -> p (a n)").bitcast(I32)

        w2_planes = keep.tile([P, E * PASSES, H], U8, name="w2_planes", align_bytes=64)
        w1_planes = keep.tile([P, E, K], U8, name="w1_planes", align_bytes=64)
        warm = keep.tile([P, 1], F32, name="warm")
        zero = keep.tile([P, 1], F32, name="zero")
        warmed = keep.tile([P, 1], F32, name="warmed")
        gates = keep.tile([P, S], F32, name="gates")
        identity = keep.tile([P, P], F32, name="identity")
        dy = [[keep.tile([P, T], F32, name=f"dy{s}{t}") for t in range(4)] for s in range(PASSES)]
        windows = [keep.tile([P, T], F32, name=f"window{k}") for k in range(K_TILES)]
        w2 = keep.tile([P, E * PASSES, 2 * H], U8, name="w2", align_bytes=64)
        w1 = keep.tile([P, E, 2 * K], U8, name="w1", align_bytes=64)
        a_sb = keep.tile([P, 4, S], F32, name="a_sb")

        dy_rows = dyT.rearrange("(s p t) w -> s t p w", p=P, t=4)

        def load_dy(s, rows=range(4)):
            for t in rows:
                nc.sync.dma_start(out=dy[s][t][:], in_=dy_rows[s, t])

        nc.sync.dma_start(offsets[:], offs)
        nc.sync.dma_start(out=gates[:, 0:C], in_=gate[0:P, 0:C])
        load_dy(0, [0])
        nc.sync.dma_start(out=gates[:, C:S], in_=gate[0:P, C:S])
        load_dy(0, [1, 2, 3])
        load_dy(1, [0, 1])
        nc.sync.dma_start(out=a_sb[:], in_=a.rearrange("(b p) c -> p b c", p=P))
        load_dy(1, [2, 3])
        load_dy(2)
        load_dy(3)

        nc.gpsimd.memset(warm[:], 0.0)
        nc.scalar.activation(warmed[:], warm[:], SIGMOID)
        make_identity(nc, identity[:])
        nc.vector.memset(flat_i32(w2_planes), 0)
        nc.vector.memset(flat_i32(w1_planes), 0)
        for k in range(K_TILES):
            nc.vector.memset(windows[k][:], 0.0)

        w2_planes_i32 = flat_i32(w2_planes).rearrange("p (a n) -> p a n", a=E * PASSES)
        w1_planes_i32 = flat_i32(w1_planes).rearrange("p (a n) -> p a n", a=E)
        w2_rows = w2_scales.rearrange("e s f i -> f (e s) i")
        w1_rows = w1_scales.rearrange("e s f i -> f (e s) i")
        for q in range(4):
            nc.sync.dma_start(out=w2_planes_i32[32 * q : 32 * q + 4], in_=w2_rows[4 * q : 4 * q + 4].bitcast(I32))
        for q in range(4):
            nc.sync.dma_start(out=w1_planes_i32[32 * q : 32 * q + 4], in_=w1_rows[4 * q : 4 * q + 4].bitcast(I32))
        w2_i32 = flat_i32(w2).rearrange("p (a n) -> p a n", a=E * PASSES)
        for e in range(E):
            nc.sync.dma_start(
                out=w2_i32[:, e * PASSES : (e + 1) * PASSES, :],
                in_=w2_words[e].rearrange("s p b -> p s b").bitcast(I32),
            )
        nc.sync.dma_start(
            out=flat_i32(w1).rearrange("p (a n) -> p a n", a=E),
            in_=w1_words.rearrange("e s p b -> p (e s) b").bitcast(I32),
        )

        g = [keep.tile([P, 4, S], F32, name=f"g{s}") for s in range(PASSES)]
        g_bf = [keep.tile([P, S, 4], BF16, name=f"g_bf{s}", align_bytes=64) for s in range(PASSES)]
        g_codes = [keep.tile([P, S], U32, name=f"g_codes{s}", align_bytes=64) for s in range(PASSES)]
        g_planes = [keep.tile([P, S], U8, name=f"g_planes{s}", align_bytes=64) for s in range(PASSES)]
        dh = [sums.tile([P, H], F32, name=f"dh{b}") for b in range(BLOCKS)]

        def gather(s, lo, hi, tiles=range(4)):
            for t in tiles:
                nc.vector.tensor_tensor(
                    g[s][:, t, lo:hi],
                    dy[s][t][:].indirect(offsets[:, lo // 16 : hi // 16]),
                    gates[:, lo:hi],
                    MULT,
                )

        def interleave(s, lo, hi):
            nc.scalar.copy(
                g_bf[s][:, lo:hi, :].rearrange("p (c i) t -> p c t i", i=4),
                g[s][:, :, lo:hi].rearrange("p t (c i) -> p c t i", i=4),
            )

        def first_product(s, lo, hi):
            nc.vector.quantize_mx(
                out=g_codes[s][:, lo:hi].bitcast(FP8X4),
                scales=g_planes[s][:, lo:hi],
                in_=g_bf[s][:, lo:hi, :].rearrange("p c t -> p (c t)"),
            )
            for b in range(lo // P, hi // P):
                e = b * P // C
                nc.tensor.matmul_mx(
                    out=dh[b][:],
                    lhsT=g_codes[s][:, b * P : (b + 1) * P].bitcast(FP8X4),
                    lhsT_scale=g_planes[s][:, b * P : (b + 1) * P],
                    rhs=w2[:, e * PASSES + s, :].bitcast(FP4X4),
                    rhs_scale=w2_planes[:, e * PASSES + s, :],
                    start=(s == 0),
                    stop=(s == PASSES - 1),
                )

        r = [keep.tile([P, H], F32, name=f"sig{b}") for b in range(BLOCKS)]
        w = [keep.tile([P, H], F32, name=f"silu{b}") for b in range(BLOCKS)]
        m = [keep.tile([P, H], F32, name=f"mix{b}") for b in range(BLOCKS)]
        aT = []

        def derivative_functions():
            for b in range(BLOCKS):
                turned = work.tile([P, 512], F32, name="turned")
                aT.append(turned)
                for i in range(4):
                    nc.tensor.transpose(turned[:, i * P : (i + 1) * P], a_sb[:, i, b * P : (b + 1) * P], identity[:])
                nc.scalar.activation(r[b][:], turned[:], SIGMOID)
            nc.scalar.activation(zero[:], r[BLOCKS - 1][:, 0:1], COPY, scale=0.0)
            for b in range(BLOCKS):
                nc.scalar.activation(w[b][:], aT[b][:], SILU, scale=-1.0, bias=zero[:])

        def derivative_products(lo, hi):
            for b in range(lo, hi):
                nc.vector.scalar_tensor_tensor(m[b][:], w[b][:], 1.0, r[b][:], SUBTRACT, MULT)

        da = [keep.tile([P, H], BF16, name=f"da{b}", align_bytes=64) for b in range(BLOCKS)]
        da_bf = keep.tile([P, S, 4], BF16, name="da_bf", align_bytes=64)
        da_codes = keep.tile([P, S], U32, name="da_codes", align_bytes=64)
        da_planes = keep.tile([P, S], U8, name="da_planes", align_bytes=64)
        dx = [keep.tile([P, S], F32, name=f"dx{k}") for k in range(K_TILES)]

        def hidden_gradient(b):
            nc.vector.scalar_tensor_tensor(da[b][:], dh[b][:], -1.0, m[b][:], MULT, MULT)
            turned = work.tile([P, 512], F32, name="turned")
            words = da[b][:].bitcast(F32)
            for u in range(2):
                nc.tensor.transpose(turned[:, u * P : (u + 1) * P], words[:, u : 2 * P : 2], identity[:])
            nc.scalar.copy(
                da_bf[:, b * P : (b + 1) * P, :].rearrange("p c t -> p (c t)").bitcast(F32).rearrange("p (r u) -> p r u", u=2),
                turned[:, 0 : 2 * P].rearrange("p (u r) -> p r u", u=2),
            )

        def second_product(lo, hi):
            e = lo // C
            nc.vector.quantize_mx(
                out=da_codes[:, lo:hi].bitcast(FP8X4),
                scales=da_planes[:, lo:hi],
                in_=da_bf[:, lo:hi, :].rearrange("p c t -> p (c t)"),
            )
            for k in range(K_TILES):
                product = work.tile([P, 512], F32, name="turned")
                nc.tensor.matmul_mx(
                    out=product[:, 0 : hi - lo],
                    lhsT=w1[:, e, 2 * P * k : 2 * P * (k + 1)].bitcast(FP4X4),
                    lhsT_scale=w1_planes[:, e, P * k : P * (k + 1)],
                    rhs=da_codes[:, lo:hi].bitcast(FP8X4),
                    rhs_scale=da_planes[:, lo:hi],
                    start=True,
                    stop=True,
                )
                nc.scalar.copy(dx[k][:, lo:hi], product[:, 0 : hi - lo])

        def scatter(lo, hi, k):
            nc.vector.tensor_copy(windows[k][:].indirect(offsets[:, lo // 16 : hi // 16]), dx[k][:, lo:hi])

        gather(0, 0, C, [0])
        gather(0, C, S, [0])
        gather(0, 0, S, [1, 2, 3])
        interleave(0, 0, S)
        derivative_functions()
        gather(1, 0, S)
        interleave(1, 0, S)
        first_product(0, 0, S)
        gather(2, 0, S)
        interleave(2, 0, S)
        first_product(1, 0, S)
        gather(3, 0, C)
        interleave(3, 0, C)
        first_product(2, 0, S)
        first_product(3, 0, C)
        derivative_products(0, 2)
        hidden_gradient(0)
        hidden_gradient(1)
        second_product(0, C)
        gather(3, C, S)
        interleave(3, C, S)
        first_product(3, C, S)
        derivative_products(2, 4)
        hidden_gradient(2)
        hidden_gradient(3)
        second_product(C, S)
        for k in range(K_TILES):
            scatter(0, C, k)
        for k in range(K_TILES):
            scatter(C, S, k)
            nc.sync.dma_start(out=out[k * P : (k + 1) * P, :], in_=windows[k][:])
